import numpy as np
import ml_dtypes


def mxq(x, axis, fmt="e4m3"):
    dtype, down = {"e4m3": (ml_dtypes.float8_e4m3fn, 7), "e5m2": (ml_dtypes.float8_e5m2, 14)}[fmt]
    v = np.moveaxis(np.asarray(x, np.float32).astype(ml_dtypes.bfloat16).astype(np.float64), axis, -1)
    blocks = v.reshape(v.shape[:-1] + (-1, 32))
    amax = np.abs(blocks).max(-1, keepdims=True)
    byte = np.maximum(np.where(amax > 0, np.frexp(amax)[1] - 1 + 127, 0) - down, 1)
    scale = np.exp2(byte - 127.0)
    codes = (blocks / scale).astype(np.float32).astype(dtype).astype(np.float64)
    return np.moveaxis((codes * scale).reshape(v.shape), -1, axis)


WIDE = False


def mx_kscale(k):
    if not WIDE:
        return np.ones(k)
    levels = np.array([10, -10, 5, -5, 0])
    if k % 512:
        return np.exp2(np.random.permutation(np.resize(levels, k // 32))).repeat(32)
    a = np.empty((k // 512, 16))
    for p in range(k // 512):
        a[p, :8] = np.random.permutation(np.resize(levels, 8))
        for g in range(8):
            far = levels[np.abs(levels - a[p, g]) >= 10]
            a[p, g + 8] = far[np.random.randint(len(far))]
    return np.exp2(a.ravel()).repeat(32)


def f64(x):
    return np.asarray(x).astype(np.float64)


def striped(idx):
    return np.tile(idx.reshape(-1, 16).T, (8, 1)).astype(np.uint16)


def unstriped(offs):
    return offs[:16].T.reshape(-1).astype(np.int64)


E2M1 = np.array([0.0, 0.5, 1.0, 1.5, 2.0, 3.0, 4.0, 6.0, -0.0, -0.5, -1.0, -1.5, -2.0, -3.0, -4.0, -6.0])


def pack_weight(w, fmt):
    k, n = w.shape
    w = f64(np.asarray(w, np.float32).astype(ml_dtypes.bfloat16)).reshape(k // 32, 32, n)
    amax = np.abs(w).max(1)
    if fmt == "e4m3":
        byte = np.frexp(amax)[1] - 1 + 127 - 7
    else:
        mant, ex = np.frexp(amax / 6.0)
        byte = np.where(mant > 0.5, ex, ex - 1) + 127
    byte = np.clip(np.where(amax > 0, byte, 1), 1, 254)
    scaled = (w * np.exp2(127.0 - byte)[:, None, :]).reshape(k, n).astype(np.float32)
    by_word = np.ascontiguousarray(scaled.reshape(k // 512, 128, 4, n).transpose(0, 1, 3, 2))
    if fmt == "e4m3":
        words = by_word.astype(ml_dtypes.float8_e4m3fn).view(np.uint8)
    else:
        c = by_word.astype(ml_dtypes.float4_e2m1fn).view(np.uint8) & 0xF
        words = (c[..., 0::2] | (c[..., 1::2] << 4)).reshape(k // 512, 128, 2 * n)
    return np.ascontiguousarray(words), np.ascontiguousarray(byte.astype(np.uint8).reshape(k // 512, 16, n))


def unpack_weight(words, scales, fmt):
    g, _, n = scales.shape
    words = np.ascontiguousarray(words).reshape(g, 128, n, -1)
    if fmt == "e4m3":
        vals = words.view(ml_dtypes.float8_e4m3fn).astype(np.float64)
    else:
        nib = np.empty((g, 128, n, 4), np.uint8)
        nib[..., 0::2] = words & 0xF
        nib[..., 1::2] = words >> 4
        vals = E2M1[nib]
    vals = vals * np.repeat(np.exp2(scales.astype(np.float64) - 127.0), 8, axis=1)[..., None]
    return vals.transpose(0, 1, 3, 2).reshape(g * 512, n)


def pack_table(v):
    words, scales = pack_weight(v, "e4m3")
    return np.concatenate([words.reshape(words.shape[0], -1), scales.reshape(scales.shape[0], -1)], axis=1)


def unpack_table(tab):
    g, t = tab.shape[0], tab.shape[1] // 528
    return unpack_weight(tab[:, :512 * t].reshape(g, 128, t, 4), tab[:, 512 * t:].reshape(g, 16, t), "e4m3")


def silu(v):
    return v / (1.0 + np.exp(-np.maximum(v, -700.0)))


G, K, M, T, S = 5, 512, 1024, 4096, 512


def setup_inputs():
    n = np.random.standard_normal
    s = mx_kscale(K)[:, None]
    return {
        "tab": pack_table(n((K, T)) * s),
        "w": (n((K, M)) / np.sqrt(K) / s).astype(np.float32),
        "b": (0.3 * n(1024)).astype(np.float32),
        "offs": striped(np.concatenate([np.random.permutation(T)[:S] for _ in range(G)])),
    }


def reference(tab, w, b, offs):
    tab_ = unpack_table(tab)[:, unstriped(offs).reshape(G, S)].sum(1)
    w_ = mxq(f64(w), 0, "e4m3")
    y = tab_.T @ w_
    return silu(y + f64(b)[None, :])

@@ -1,0 +1,179 @@
+from contextlib import ExitStack
+
+import concourse.mybir as mybir
+from concourse.masks import make_identity
+
+G, K, M, T, S = 5, 512, 1024, 4096, 512
+FLOPS = 2 * G * K * M * S
+
+F32 = mybir.dt.float32
+BF16 = mybir.dt.bfloat16
+I32 = mybir.dt.int32
+U32 = mybir.dt.uint32
+U16 = mybir.dt.uint16
+U8 = mybir.dt.uint8
+FP8X4 = mybir.dt.float8_e4m3fn_x4
+SILU = mybir.ActivationFunctionType.Silu
+ADD = mybir.AluOpType.add
+
+P = 128
+PACK = 4
+BANK = 512
+CHUNK = 256
+LIST_COLS = S // 16
+
+
+def tile_list_tabbag_tm_silu_kernel(tc, tab, w, b, offs, out):
+    nc = tc.nc
+    with ExitStack() as ctx:
+        keep = ctx.enter_context(tc.tile_pool(name="keep", bufs=1))
+        psum = ctx.enter_context(tc.psum_pool(name="psum", bufs=1))
+
+        def sb(name, shape, dtype, tag=None):
+            return keep.tile(shape, dtype, name=name, tag=tag or name, align_bytes=64)
+
+        offsets = keep.tile([P, G * LIST_COLS], U16, name="offsets")
+        nc.sync.dma_start(offsets[:], offs)
+
+        table_scales = sb("table_scales", [P, T], U8)
+        nc.vector.memset(table_scales[:].bitcast(I32), 0)
+        ident = sb("ident", [P, P], F32)
+        nc.vector.memset(ident[:], 0.0)
+        make_identity(nc, ident[:], nomemset=True)
+        scale_rows = tab[0, K * T :].rearrange("(q t) -> q t", t=T).bitcast(I32)
+        per = M // P
+        b_cols = sb("b_cols", [P, per], F32)
+        nc.sync.dma_start(b_cols[:], b.rearrange("(p c) -> p c", c=per))
+
+        w_rows = w.rearrange("(p i) n -> p i n", i=PACK)
+        w_codes = sb("w_codes", [P, M], U32)
+        w_scales = sb("w_scales", [P, M], U8)
+
+        def load_w(c0, c1, tag):
+            raw = sb("w_raw%d" % c0, [P, PACK, (c1 - c0) * CHUNK], F32, tag)
+            nc.sync.dma_start(raw[:], w_rows[:, :, c0 * CHUNK : c1 * CHUNK])
+            return [raw[:, :, c * CHUNK : (c + 1) * CHUNK] for c in range(c1 - c0)]
+
+        def round_w(raw, rounded):
+            nc.scalar.copy(
+                rounded.rearrange("p (n m i) -> p n i m", m=4, i=PACK),
+                raw.rearrange("p i (n m) -> p n i m", m=4),
+            )
+
+        def quantize_w(n0, n1, rounded):
+            cols = slice(n0, n1)
+            nc.vector.quantize_mx(out=w_codes[:, cols].bitcast(FP8X4), scales=w_scales[:, cols], in_=rounded[:])
+
+        codes = {}
+        scales = {}
+
+        def gather_scales(g0, g1, tag):
+            picked = sb("picked_scales%d" % g0, [P, (g1 - g0) * S], U8, tag)
+            nc.vector.tensor_copy(picked[:], table_scales[:].indirect(offsets[:, g0 * LIST_COLS : g1 * LIST_COLS]))
+            for g in range(g0, g1):
+                scales[g] = picked[:, (g - g0) * S : (g - g0 + 1) * S]
+
+        def gather_words(g, tag):
+            picked = sb("picked_words%d" % g, [P, S], U32, tag)
+            nc.vector.tensor_copy(picked[:], table_words[:].indirect(offsets[:, g * LIST_COLS : (g + 1) * LIST_COLS]))
+            codes[g] = picked[:]
+
+        for quad in range(4):
+            nc.sync.dma_start(
+                table_scales[32 * quad : 32 * quad + 4, :].bitcast(I32), scale_rows[4 * quad : 4 * quad + 4, :]
+            )
+        (raw0,) = load_w(0, 1, "slot_a")
+        table_words = sb("table_words", [P, T], U32)
+        nc.sync.dma_start(table_words[:].bitcast(I32), tab[0, : K * T].rearrange("(p c) -> p c", p=P).bitcast(I32))
+        (raw1,) = load_w(1, 2, "slot_b")
+
+        bias = sb("bias", [P, M], F32)
+
+        gather_scales(0, 4, None)
+        bf0 = sb("bf0", [P, CHUNK * PACK], BF16)
+        round_w(raw0, bf0[:])
+        quantize_w(0, CHUNK, bf0)
+        raw2, raw3 = load_w(2, 4, "slot_a")
+
+        for half in range(2):
+            spread = psum.tile([P, 4, P], F32, name="spread%d" % half, tag="bank%d" % (6 + half))
+            for c in range(4):
+                col = 4 * half + c
+                nc.tensor.transpose(spread[:, c, :], b_cols[:, col : col + 1].to_broadcast([P, P]), ident[:])
+            nc.scalar.copy(
+                bias[:].rearrange("j (p c) -> j p c", c=per)[:, :, 4 * half : 4 * half + 4],
+                spread[:].rearrange("j c p -> j p c"),
+            )
+
+        banks = [psum.tile([P, BANK], F32, name="acc%d" % i, tag="bank%d" % i) for i in range(8)]
+
+        def multiply(acc, first, g, jt, n0, n1):
+            places = slice(jt * P, (jt + 1) * P)
+            nc.tensor.matmul_mx(
+                out=acc,
+                lhsT=codes[g][:, places].bitcast(FP8X4),
+                lhsT_scale=scales[g][:, places],
+                rhs=w_codes[:, n0:n1].bitcast(FP8X4),
+                rhs_scale=w_scales[:, n0:n1],
+                start=first,
+                stop=(g == G - 1),
+            )
+
+        def into_bank(g, jt, n0, n1):
+            half = n0 // BANK
+            acc = banks[4 * half + jt][:, n0 - half * BANK : n1 - half * BANK]
+            multiply(acc, g == 0 and n0 % BANK == 0, g, jt, n0, n1)
+
+        def multiply_chunk(gs, n0, n1):
+            for g in gs:
+                for jt in range(4):
+                    into_bank(g, jt, n0, n1)
+
+        def finish(acc, jt, n0, n1):
+            pre = sb("pre%d_%d" % (jt, n0), [P, n1 - n0], F32)
+            nc.vector.tensor_tensor(pre[:], acc, bias[:, n0:n1], ADD)
+            res = sb("res%d_%d" % (jt, n0), [P, n1 - n0], F32)
+            nc.scalar.activation(res[:], pre[:], SILU)
+            nc.sync.dma_start(out[jt * P : (jt + 1) * P, n0:n1], res[:])
+
+        gather_words(0, None)
+        multiply_chunk([0], 0, CHUNK)
+        gather_words(1, None)
+        multiply_chunk([1], 0, CHUNK)
+        bf1 = sb("bf1", [P, CHUNK * PACK], BF16, "slot_d")
+        round_w(raw1, bf1[:])
+        quantize_w(CHUNK, BANK, bf1)
+        multiply_chunk([0, 1], CHUNK, BANK)
+        gather_words(2, "slot_d")
+        multiply_chunk([2], 0, BANK)
+        gather_words(3, "slot_b")
+        multiply_chunk([3], 0, BANK)
+        bf23 = sb("bf23", [P, BANK * PACK], BF16, "slot_f")
+        round_w(raw2, bf23[:, : CHUNK * PACK])
+        round_w(raw3, bf23[:, CHUNK * PACK :])
+        quantize_w(BANK, M, bf23)
+        gather_scales(4, 5, "slot_a")
+        gather_words(4, "slot_f")
+
+        def close(half, jt):
+            into_bank(G - 1, jt, half * BANK, (half + 1) * BANK)
+            finish(banks[4 * half + jt][:], jt, half * BANK, (half + 1) * BANK)
+
+        for g in range(G - 1):
+            into_bank(g, 0, BANK, M)
+        close(0, 0)
+        close(0, 1)
+        for jt, closing in ((1, ((0, 2), (0, 3))), (2, ((1, 0), (1, 1)))):
+            for pair in range(2):
+                into_bank(2 * pair, jt, BANK, M)
+                into_bank(2 * pair + 1, jt, BANK, M)
+                close(*closing[pair])
+        for g in range(G - 1):
+            into_bank(g, 3, BANK, BANK + CHUNK)
+        close(1, 2)
+        into_bank(G - 1, 3, BANK, BANK + CHUNK)
+        finish(banks[7][:, :CHUNK], 3, BANK, BANK + CHUNK)
+        last = psum.tile([P, CHUNK], F32, name="last", tag="bank0")
+        for g in range(G):
+            multiply(last[:], g == 0, g, 3, BANK + CHUNK, M)
+        finish(last[:], 3, BANK + CHUNK, M)

@@ -27,16 +27,20 @@ def tile_list_tabbag_tm_silu_kernel(tc, tab, w, b, offs, out):
     nc = tc.nc
     with ExitStack() as ctx:
         keep = ctx.enter_context(tc.tile_pool(name="keep", bufs=1))
+        shared = ctx.enter_context(tc.tile_pool(name="shared", bufs=1))
         psum = ctx.enter_context(tc.psum_pool(name="psum", bufs=1))
 
         def sb(name, shape, dtype, tag=None):
+            if isinstance(tag, int):
+                return shared.tile(shape, dtype, name=name, offset=tag, align_bytes=64)
             return keep.tile(shape, dtype, name=name, tag=tag or name, align_bytes=64)
 
         offsets = keep.tile([P, G * LIST_COLS], U16, name="offsets")
         nc.sync.dma_start(offsets[:], offs)
 
         table_scales = sb("table_scales", [P, T], U8)
-        nc.vector.memset(table_scales[:].bitcast(I32), 0)
+        nc.gpsimd.memset(table_scales[:, : T // 2].bitcast(I32), 0)
+        nc.vector.memset(table_scales[:, T // 2 :].bitcast(I32), 0)
         ident = sb("ident", [P, P], F32)
         nc.vector.memset(ident[:], 0.0)
         make_identity(nc, ident[:], nomemset=True)
@@ -49,15 +53,20 @@ def tile_list_tabbag_tm_silu_kernel(tc, tab, w, b, offs, out):
         w_codes = sb("w_codes", [P, M], U32)
         w_scales = sb("w_scales", [P, M], U8)
 
-        def load_w(c0, c1, tag):
-            raw = sb("w_raw%d" % c0, [P, PACK, (c1 - c0) * CHUNK], F32, tag)
-            nc.sync.dma_start(raw[:], w_rows[:, :, c0 * CHUNK : c1 * CHUNK])
-            return [raw[:, :, c * CHUNK : (c + 1) * CHUNK] for c in range(c1 - c0)]
+        def load_w(n0, n1):
+            raw = sb("w_raw%d" % n0, [P, PACK, n1 - n0], F32, 16 * n0)
+            nc.sync.dma_start(raw[:], w_rows[:, :, n0:n1])
+            return raw
+
+        def prepare_w(n0, n1, raw):
+            rounded = sb("w_bf%d" % n0, [P, (n1 - n0) * PACK], BF16)
+            round_w(raw[:], rounded[:])
+            quantize_w(n0, n1, rounded)
 
         def round_w(raw, rounded):
             nc.scalar.copy(
-                rounded.rearrange("p (n m i) -> p n i m", m=4, i=PACK),
-                raw.rearrange("p i (n m) -> p n i m", m=4),
+                rounded.rearrange("p (n i) -> p n i", i=PACK),
+                raw.rearrange("p i n -> p n i"),
             )
 
         def quantize_w(n0, n1, rounded):
@@ -78,22 +87,16 @@ def tile_list_tabbag_tm_silu_kernel(tc, tab, w, b, offs, out):
             nc.vector.tensor_copy(picked[:], table_words[:].indirect(offsets[:, g * LIST_COLS : (g + 1) * LIST_COLS]))
             codes[g] = picked[:]
 
-        for quad in range(4):
-            nc.sync.dma_start(
-                table_scales[32 * quad : 32 * quad + 4, :].bitcast(I32), scale_rows[4 * quad : 4 * quad + 4, :]
-            )
-        (raw0,) = load_w(0, 1, "slot_a")
+        for r in range(4):
+            nc.sync.dma_start(table_scales[r:P:32, :].bitcast(I32), scale_rows[r:16:4, :])
         table_words = sb("table_words", [P, T], U32)
         nc.sync.dma_start(table_words[:].bitcast(I32), tab[0, : K * T].rearrange("(p c) -> p c", p=P).bitcast(I32))
-        (raw1,) = load_w(1, 2, "slot_b")
+        edges = (0, 128, 256, 512, 1024)
+        raws = [load_w(edges[c], edges[c + 1]) for c in range(4)]
 
         bias = sb("bias", [P, M], F32)
 
         gather_scales(0, 4, None)
-        bf0 = sb("bf0", [P, CHUNK * PACK], BF16)
-        round_w(raw0, bf0[:])
-        quantize_w(0, CHUNK, bf0)
-        raw2, raw3 = load_w(2, 4, "slot_a")
 
         for half in range(2):
             spread = psum.tile([P, 4, P], F32, name="spread%d" % half, tag="bank%d" % (6 + half))
@@ -137,23 +140,21 @@ def tile_list_tabbag_tm_silu_kernel(tc, tab, w, b, offs, out):
             nc.sync.dma_start(out[jt * P : (jt + 1) * P, n0:n1], res[:])
 
         gather_words(0, None)
-        multiply_chunk([0], 0, CHUNK)
-        gather_words(1, None)
-        multiply_chunk([1], 0, CHUNK)
-        bf1 = sb("bf1", [P, CHUNK * PACK], BF16, "slot_d")
-        round_w(raw1, bf1[:])
-        quantize_w(CHUNK, BANK, bf1)
-        multiply_chunk([0, 1], CHUNK, BANK)
-        gather_words(2, "slot_d")
-        multiply_chunk([2], 0, BANK)
-        gather_words(3, "slot_b")
+        prepare_w(edges[0], edges[1], raws[0])
+        multiply_chunk([0], edges[0], edges[1])
+        gather_words(1, 16 * edges[0])
+        multiply_chunk([1], edges[0], edges[1])
+        prepare_w(edges[1], edges[2], raws[1])
+        multiply_chunk([0, 1], edges[1], edges[2])
+        gather_words(2, 16 * edges[1])
+        multiply_chunk([2], edges[0], edges[2])
+        prepare_w(edges[2], edges[3], raws[2])
+        multiply_chunk([0, 1, 2], edges[2], edges[3])
+        gather_words(3, 16 * edges[2])
         multiply_chunk([3], 0, BANK)
-        bf23 = sb("bf23", [P, BANK * PACK], BF16, "slot_f")
-        round_w(raw2, bf23[:, : CHUNK * PACK])
-        round_w(raw3, bf23[:, CHUNK * PACK :])
-        quantize_w(BANK, M, bf23)
-        gather_scales(4, 5, "slot_a")
-        gather_words(4, "slot_f")
+        gather_scales(4, 5, 16 * edges[2] + 4 * S)
+        prepare_w(edges[3], edges[4], raws[3])
+        gather_words(4, 16 * edges[3])
 
         def close(half, jt):
             into_bank(G - 1, jt, half * BANK, (half + 1) * BANK)

@@ -19,162 +19,170 @@ ADD = mybir.AluOpType.add
 P = 128
 PACK = 4
 BANK = 512
-CHUNK = 256
-LIST_COLS = S // 16
+TILES = S // P
+GROUP = 16
+
+EDGES = (0, 128, 256, 512, 768, 1024)
+EARLY = 1920
+ZEROED_BY_GPSIMD = 2688
+LAST = 128
 
 
 def tile_list_tabbag_tm_silu_kernel(tc, tab, w, b, offs, out):
     nc = tc.nc
     with ExitStack() as ctx:
         keep = ctx.enter_context(tc.tile_pool(name="keep", bufs=1))
-        shared = ctx.enter_context(tc.tile_pool(name="shared", bufs=1))
+        staged = ctx.enter_context(tc.tile_pool(name="staged", bufs=1))
         psum = ctx.enter_context(tc.psum_pool(name="psum", bufs=1))
 
-        def sb(name, shape, dtype, tag=None):
-            if isinstance(tag, int):
-                return shared.tile(shape, dtype, name=name, offset=tag, align_bytes=64)
-            return keep.tile(shape, dtype, name=name, tag=tag or name, align_bytes=64)
+        def sb(name, shape, dtype, at=None):
+            if at is None:
+                return keep.tile(shape, dtype, name=name, align_bytes=64)
+            return staged.tile(shape, dtype, name=name, offset=at, align_bytes=64)
 
-        offsets = keep.tile([P, G * LIST_COLS], U16, name="offsets")
+        def chunk_at(c):
+            return 4 * PACK * EDGES[c]
+
+        offsets = keep.tile([P, G * S // GROUP], U16, name="offsets")
         nc.sync.dma_start(offsets[:], offs)
 
         table_scales = sb("table_scales", [P, T], U8)
-        nc.gpsimd.memset(table_scales[:, : T // 2].bitcast(I32), 0)
-        nc.vector.memset(table_scales[:, T // 2 :].bitcast(I32), 0)
+        nc.gpsimd.memset(table_scales[:, :ZEROED_BY_GPSIMD].bitcast(I32), 0)
+        nc.vector.memset(table_scales[:, ZEROED_BY_GPSIMD:].bitcast(I32), 0)
         ident = sb("ident", [P, P], F32)
         nc.vector.memset(ident[:], 0.0)
         make_identity(nc, ident[:], nomemset=True)
-        scale_rows = tab[0, K * T :].rearrange("(q t) -> q t", t=T).bitcast(I32)
-        per = M // P
-        b_cols = sb("b_cols", [P, per], F32)
-        nc.sync.dma_start(b_cols[:], b.rearrange("(p c) -> p c", c=per))
+
+        b_run = M // P
+        b_cols = sb("b_cols", [P, b_run], F32)
+        nc.scalar.dma_start(b_cols[:], b.rearrange("(p c) -> p c", c=b_run))
 
         w_rows = w.rearrange("(p i) n -> p i n", i=PACK)
-        w_codes = sb("w_codes", [P, M], U32)
-        w_scales = sb("w_scales", [P, M], U8)
 
-        def load_w(n0, n1):
-            raw = sb("w_raw%d" % n0, [P, PACK, n1 - n0], F32, 16 * n0)
-            nc.sync.dma_start(raw[:], w_rows[:, :, n0:n1])
+        def load_w(c):
+            raw = sb("w_raw%d" % c, [P, PACK, EDGES[c + 1] - EDGES[c]], F32, chunk_at(c))
+            nc.sync.dma_start(raw[:], w_rows[:, :, EDGES[c] : EDGES[c + 1]])
             return raw
 
-        def prepare_w(n0, n1, raw):
-            rounded = sb("w_bf%d" % n0, [P, (n1 - n0) * PACK], BF16)
-            round_w(raw[:], rounded[:])
-            quantize_w(n0, n1, rounded)
-
-        def round_w(raw, rounded):
-            nc.scalar.copy(
-                rounded.rearrange("p (n i) -> p n i", i=PACK),
-                raw.rearrange("p i n -> p n i"),
-            )
-
-        def quantize_w(n0, n1, rounded):
-            cols = slice(n0, n1)
-            nc.vector.quantize_mx(out=w_codes[:, cols].bitcast(FP8X4), scales=w_scales[:, cols], in_=rounded[:])
-
-        codes = {}
-        scales = {}
-
-        def gather_scales(g0, g1, tag):
-            picked = sb("picked_scales%d" % g0, [P, (g1 - g0) * S], U8, tag)
-            nc.vector.tensor_copy(picked[:], table_scales[:].indirect(offsets[:, g0 * LIST_COLS : g1 * LIST_COLS]))
-            for g in range(g0, g1):
-                scales[g] = picked[:, (g - g0) * S : (g - g0 + 1) * S]
-
-        def gather_words(g, tag):
-            picked = sb("picked_words%d" % g, [P, S], U32, tag)
-            nc.vector.tensor_copy(picked[:], table_words[:].indirect(offsets[:, g * LIST_COLS : (g + 1) * LIST_COLS]))
-            codes[g] = picked[:]
-
+        scale_rows = tab[0, K * T :].rearrange("(q t) -> q t", t=T).bitcast(I32)
         for r in range(4):
             nc.sync.dma_start(table_scales[r:P:32, :].bitcast(I32), scale_rows[r:16:4, :])
+        raws = [load_w(0)]
         table_words = sb("table_words", [P, T], U32)
         nc.sync.dma_start(table_words[:].bitcast(I32), tab[0, : K * T].rearrange("(p c) -> p c", p=P).bitcast(I32))
-        edges = (0, 128, 256, 512, 1024)
-        raws = [load_w(edges[c], edges[c + 1]) for c in range(4)]
+        raws.extend(load_w(c) for c in range(1, len(EDGES) - 1))
+
+        w_words = sb("w_words", [P, M], U32)
+        w_scales = sb("w_scales", [P, M], U8)
+
+        def prepare_w(c):
+            cols = slice(EDGES[c], EDGES[c + 1])
+            rounded = sb("w_bf%d" % c, [P, (EDGES[c + 1] - EDGES[c]) * PACK], BF16)
+            nc.scalar.copy(rounded[:].rearrange("p (n i) -> p n i", i=PACK), raws[c][:].rearrange("p i n -> p n i"))
+            nc.vector.quantize_mx(out=w_words[:, cols].bitcast(FP8X4), scales=w_scales[:, cols], in_=rounded[:])
+
+        def gather(name, window, dtype, m0, m1, at=None):
+            picked = sb(name, [P, m1 - m0], dtype, at)
+            nc.vector.tensor_copy(picked[:], window[:].indirect(offsets[:, m0 // GROUP : m1 // GROUP]))
+            return picked
+
+        picked_words = []
+
+        def gather_words(g, at=None):
+            picked_words.append(gather("words%d" % g, table_words, U32, g * S, (g + 1) * S, at))
+
+        picked_scales = [gather("scales_early", table_scales, U8, 0, EARLY)]
+        prepare_w(0)
 
         bias = sb("bias", [P, M], F32)
-
-        gather_scales(0, 4, None)
-
-        for half in range(2):
-            spread = psum.tile([P, 4, P], F32, name="spread%d" % half, tag="bank%d" % (6 + half))
-            for c in range(4):
-                col = 4 * half + c
+        per_bank = BANK // P
+        for part in range(b_run // per_bank):
+            spread = psum.tile([P, per_bank, P], F32, name="spread%d" % part, tag="bank%d" % (2 * TILES - 2 + part))
+            for c in range(per_bank):
+                col = per_bank * part + c
                 nc.tensor.transpose(spread[:, c, :], b_cols[:, col : col + 1].to_broadcast([P, P]), ident[:])
             nc.scalar.copy(
-                bias[:].rearrange("j (p c) -> j p c", c=per)[:, :, 4 * half : 4 * half + 4],
+                bias[:].rearrange("j (p c) -> j p c", c=b_run)[:, :, per_bank * part : per_bank * (part + 1)],
                 spread[:].rearrange("j c p -> j p c"),
             )
 
-        banks = [psum.tile([P, BANK], F32, name="acc%d" % i, tag="bank%d" % i) for i in range(8)]
+        banks = [psum.tile([P, BANK], F32, name="acc%d" % i, tag="bank%d" % i) for i in range(2 * TILES)]
 
-        def multiply(acc, first, g, jt, n0, n1):
-            places = slice(jt * P, (jt + 1) * P)
+        def multiply(acc, g, t, n0, n1, opens, closes):
+            m = g * S + t * P
+            plane = picked_scales[0][:, m : m + P] if m < EARLY else picked_scales[1][:, m - EARLY : m - EARLY + P]
             nc.tensor.matmul_mx(
                 out=acc,
-                lhsT=codes[g][:, places].bitcast(FP8X4),
-                lhsT_scale=scales[g][:, places],
-                rhs=w_codes[:, n0:n1].bitcast(FP8X4),
+                lhsT=picked_words[g][:, t * P : (t + 1) * P].bitcast(FP8X4),
+                lhsT_scale=plane,
+                rhs=w_words[:, n0:n1].bitcast(FP8X4),
                 rhs_scale=w_scales[:, n0:n1],
-                start=first,
-                stop=(g == G - 1),
+                start=opens,
+                stop=closes,
             )
 
-        def into_bank(g, jt, n0, n1):
+        def into_bank(g, t, n0, n1, closes=False):
             half = n0 // BANK
-            acc = banks[4 * half + jt][:, n0 - half * BANK : n1 - half * BANK]
-            multiply(acc, g == 0 and n0 % BANK == 0, g, jt, n0, n1)
+            acc = banks[TILES * half + t][:, n0 - half * BANK : n1 - half * BANK]
+            multiply(acc, g, t, n0, n1, g == 0 and n0 % BANK == 0, closes)
 
-        def multiply_chunk(gs, n0, n1):
-            for g in gs:
-                for jt in range(4):
-                    into_bank(g, jt, n0, n1)
+        def sweep(lookups, n0, n1, tiles=range(TILES)):
+            for g in lookups:
+                for t in tiles:
+                    into_bank(g, t, n0, n1)
 
-        def finish(acc, jt, n0, n1):
-            pre = sb("pre%d_%d" % (jt, n0), [P, n1 - n0], F32)
+        def finish(acc, t, n0, n1):
+            pre = sb("pre%d_%d" % (t, n0), [P, n1 - n0], F32)
             nc.vector.tensor_tensor(pre[:], acc, bias[:, n0:n1], ADD)
-            res = sb("res%d_%d" % (jt, n0), [P, n1 - n0], F32)
+            res = sb("res%d_%d" % (t, n0), [P, n1 - n0], F32)
             nc.scalar.activation(res[:], pre[:], SILU)
-            nc.sync.dma_start(out[jt * P : (jt + 1) * P, n0:n1], res[:])
+            nc.sync.dma_start(out[t * P : (t + 1) * P, n0:n1], res[:])
 
-        gather_words(0, None)
-        prepare_w(edges[0], edges[1], raws[0])
-        multiply_chunk([0], edges[0], edges[1])
-        gather_words(1, 16 * edges[0])
-        multiply_chunk([1], edges[0], edges[1])
-        prepare_w(edges[1], edges[2], raws[1])
-        multiply_chunk([0, 1], edges[1], edges[2])
-        gather_words(2, 16 * edges[1])
-        multiply_chunk([2], edges[0], edges[2])
-        prepare_w(edges[2], edges[3], raws[2])
-        multiply_chunk([0, 1, 2], edges[2], edges[3])
-        gather_words(3, 16 * edges[2])
-        multiply_chunk([3], 0, BANK)
-        gather_scales(4, 5, 16 * edges[2] + 4 * S)
-        prepare_w(edges[3], edges[4], raws[3])
-        gather_words(4, 16 * edges[3])
+        gather_words(0)
+        sweep([0], EDGES[0], EDGES[1])
+        prepare_w(1)
+        sweep([0], EDGES[1], EDGES[2])
+        gather_words(1, chunk_at(1))
+        sweep([1], EDGES[0], EDGES[2])
+        prepare_w(2)
+        sweep([0, 1], EDGES[2], EDGES[3])
+        gather_words(2, chunk_at(2))
+        sweep([2], 0, BANK)
+        prepare_w(3)
+        sweep([0, 1, 2], EDGES[3], EDGES[4])
+        gather_words(3, chunk_at(3))
+        last_tile = TILES - 1
+        sweep([3], 0, BANK, range(last_tile))
+        prepare_w(4)
+        picked_scales.append(gather("scales_late", table_scales, U8, EARLY, G * S, chunk_at(4)))
+        gather_words(4, chunk_at(4) + 4 * S)
+        sweep([3], 0, BANK, [last_tile])
 
-        def close(half, jt):
-            into_bank(G - 1, jt, half * BANK, (half + 1) * BANK)
-            finish(banks[4 * half + jt][:], jt, half * BANK, (half + 1) * BANK)
+        def close(half, t):
+            into_bank(G - 1, t, half * BANK, (half + 1) * BANK, True)
+            finish(banks[TILES * half + t][:], t, half * BANK, (half + 1) * BANK)
 
-        for g in range(G - 1):
-            into_bank(g, 0, BANK, M)
+        def catch_up(t):
+            sweep([0, 1, 2], EDGES[4], M, [t])
+            into_bank(3, t, BANK, M)
+
         close(0, 0)
         close(0, 1)
-        for jt, closing in ((1, ((0, 2), (0, 3))), (2, ((1, 0), (1, 1)))):
-            for pair in range(2):
-                into_bank(2 * pair, jt, BANK, M)
-                into_bank(2 * pair + 1, jt, BANK, M)
-                close(*closing[pair])
-        for g in range(G - 1):
-            into_bank(g, 3, BANK, BANK + CHUNK)
-        close(1, 2)
-        into_bank(G - 1, 3, BANK, BANK + CHUNK)
-        finish(banks[7][:, :CHUNK], 3, BANK, BANK + CHUNK)
-        last = psum.tile([P, CHUNK], F32, name="last", tag="bank0")
+        catch_up(0)
+        close(0, 2)
+        close(0, 3)
+        close(1, 0)
+        for t in range(1, last_tile):
+            catch_up(t)
+            close(1, t)
+
+        cut = M - LAST
+        sweep([0, 1, 2], EDGES[4], cut, [last_tile])
+        for g in (3, 4):
+            into_bank(g, last_tile, BANK, EDGES[4])
+            into_bank(g, last_tile, EDGES[4], cut, g == G - 1)
+        finish(banks[-1][:, : cut - BANK], last_tile, BANK, cut)
+        narrow = psum.tile([P, LAST], F32, name="narrow", tag="bank0")
         for g in range(G):
-            multiply(last[:], g == 0, g, 3, BANK + CHUNK, M)
-        finish(last[:], 3, BANK + CHUNK, M)
+            multiply(narrow[:], g, last_tile, cut, M, g == 0, g == G - 1)
+        finish(narrow[:], last_tile, cut, M)

@@ -23,9 +23,7 @@ TILES = S // P
 GROUP = 16
 
 EDGES = (0, 128, 256, 512, 768, 1024)
-EARLY = 1920
-ZEROED_BY_GPSIMD = 2688
-LAST = 128
+EARLY = G - 1
 
 
 def tile_list_tabbag_tm_silu_kernel(tc, tab, w, b, offs, out):
@@ -47,15 +45,15 @@ def tile_list_tabbag_tm_silu_kernel(tc, tab, w, b, offs, out):
         nc.sync.dma_start(offsets[:], offs)
 
         table_scales = sb("table_scales", [P, T], U8)
-        nc.gpsimd.memset(table_scales[:, :ZEROED_BY_GPSIMD].bitcast(I32), 0)
-        nc.vector.memset(table_scales[:, ZEROED_BY_GPSIMD:].bitcast(I32), 0)
+        nc.gpsimd.memset(table_scales[:, : T // 2].bitcast(I32), 0)
+        nc.vector.memset(table_scales[:, T // 2 :].bitcast(I32), 0)
         ident = sb("ident", [P, P], F32)
         nc.vector.memset(ident[:], 0.0)
         make_identity(nc, ident[:], nomemset=True)
 
         b_run = M // P
         b_cols = sb("b_cols", [P, b_run], F32)
-        nc.scalar.dma_start(b_cols[:], b.rearrange("(p c) -> p c", c=b_run))
+        nc.sync.dma_start(b_cols[:], b.rearrange("(p c) -> p c", c=b_run))
 
         w_rows = w.rearrange("(p i) n -> p i n", i=PACK)
 
@@ -67,10 +65,9 @@ def tile_list_tabbag_tm_silu_kernel(tc, tab, w, b, offs, out):
         scale_rows = tab[0, K * T :].rearrange("(q t) -> q t", t=T).bitcast(I32)
         for r in range(4):
             nc.sync.dma_start(table_scales[r:P:32, :].bitcast(I32), scale_rows[r:16:4, :])
-        raws = [load_w(0)]
         table_words = sb("table_words", [P, T], U32)
         nc.sync.dma_start(table_words[:].bitcast(I32), tab[0, : K * T].rearrange("(p c) -> p c", p=P).bitcast(I32))
-        raws.extend(load_w(c) for c in range(1, len(EDGES) - 1))
+        raws = [load_w(c) for c in range(len(EDGES) - 1)]
 
         w_words = sb("w_words", [P, M], U32)
         w_scales = sb("w_scales", [P, M], U8)
@@ -91,8 +88,7 @@ def tile_list_tabbag_tm_silu_kernel(tc, tab, w, b, offs, out):
         def gather_words(g, at=None):
             picked_words.append(gather("words%d" % g, table_words, U32, g * S, (g + 1) * S, at))
 
-        picked_scales = [gather("scales_early", table_scales, U8, 0, EARLY)]
-        prepare_w(0)
+        picked_scales = [gather("scales_early", table_scales, U8, 0, EARLY * S)]
 
         bias = sb("bias", [P, M], F32)
         per_bank = BANK // P
@@ -109,12 +105,11 @@ def tile_list_tabbag_tm_silu_kernel(tc, tab, w, b, offs, out):
         banks = [psum.tile([P, BANK], F32, name="acc%d" % i, tag="bank%d" % i) for i in range(2 * TILES)]
 
         def multiply(acc, g, t, n0, n1, opens, closes):
-            m = g * S + t * P
-            plane = picked_scales[0][:, m : m + P] if m < EARLY else picked_scales[1][:, m - EARLY : m - EARLY + P]
+            m = (g % EARLY) * S + t * P
             nc.tensor.matmul_mx(
                 out=acc,
                 lhsT=picked_words[g][:, t * P : (t + 1) * P].bitcast(FP8X4),
-                lhsT_scale=plane,
+                lhsT_scale=picked_scales[g // EARLY][:, m : m + P],
                 rhs=w_words[:, n0:n1].bitcast(FP8X4),
                 rhs_scale=w_scales[:, n0:n1],
                 start=opens,
@@ -138,51 +133,41 @@ def tile_list_tabbag_tm_silu_kernel(tc, tab, w, b, offs, out):
             nc.scalar.activation(res[:], pre[:], SILU)
             nc.sync.dma_start(out[t * P : (t + 1) * P, n0:n1], res[:])
 
-        gather_words(0)
-        sweep([0], EDGES[0], EDGES[1])
-        prepare_w(1)
-        sweep([0], EDGES[1], EDGES[2])
-        gather_words(1, chunk_at(1))
-        sweep([1], EDGES[0], EDGES[2])
-        prepare_w(2)
-        sweep([0, 1], EDGES[2], EDGES[3])
-        gather_words(2, chunk_at(2))
-        sweep([2], 0, BANK)
-        prepare_w(3)
-        sweep([0, 1, 2], EDGES[3], EDGES[4])
-        gather_words(3, chunk_at(3))
         last_tile = TILES - 1
-        sweep([3], 0, BANK, range(last_tile))
+        gather_words(0)
+        prepare_w(0)
+        sweep([0], EDGES[0], EDGES[1])
+        gather_words(1, chunk_at(0))
+        sweep([1], EDGES[0], EDGES[1])
+        prepare_w(1)
+        sweep([0, 1], EDGES[1], EDGES[2])
+        gather_words(2, chunk_at(1))
+        sweep([2], EDGES[0], EDGES[2])
+        prepare_w(2)
+        sweep([0, 1, 2], EDGES[2], EDGES[3])
+        gather_words(3, chunk_at(2))
+        sweep([3], 0, BANK)
+        prepare_w(3)
+        sweep(range(G - 1), EDGES[3], EDGES[4], range(last_tile))
+        picked_scales.append(gather("scales_late", table_scales, U8, EARLY * S, G * S, chunk_at(3)))
         prepare_w(4)
-        picked_scales.append(gather("scales_late", table_scales, U8, EARLY, G * S, chunk_at(4)))
-        gather_words(4, chunk_at(4) + 4 * S)
-        sweep([3], 0, BANK, [last_tile])
+        gather_words(4, chunk_at(4))
 
-        def close(half, t):
+        def close(i):
+            half, t = divmod(i, TILES)
             into_bank(G - 1, t, half * BANK, (half + 1) * BANK, True)
-            finish(banks[TILES * half + t][:], t, half * BANK, (half + 1) * BANK)
+            finish(banks[i][:], t, half * BANK, (half + 1) * BANK)
 
-        def catch_up(t):
-            sweep([0, 1, 2], EDGES[4], M, [t])
-            into_bank(3, t, BANK, M)
+        for t in range(last_tile):
+            close(2 * t)
+            close(2 * t + 1)
+            sweep(range(G - 1), EDGES[4], M, [t])
+        close(2 * last_tile)
 
-        close(0, 0)
-        close(0, 1)
-        catch_up(0)
-        close(0, 2)
-        close(0, 3)
-        close(1, 0)
-        for t in range(1, last_tile):
-            catch_up(t)
-            close(1, t)
-
-        cut = M - LAST
-        sweep([0, 1, 2], EDGES[4], cut, [last_tile])
-        for g in (3, 4):
-            into_bank(g, last_tile, BANK, EDGES[4])
-            into_bank(g, last_tile, EDGES[4], cut, g == G - 1)
-        finish(banks[-1][:, : cut - BANK], last_tile, BANK, cut)
-        narrow = psum.tile([P, LAST], F32, name="narrow", tag="bank0")
         for g in range(G):
-            multiply(narrow[:], g, last_tile, cut, M, g == 0, g == G - 1)
-        finish(narrow[:], last_tile, cut, M)
+            into_bank(g, last_tile, BANK, EDGES[4], g == G - 1)
+        finish(banks[-1][:, : EDGES[4] - BANK], last_tile, BANK, EDGES[4])
+        second = psum.tile([P, M - EDGES[4]], F32, name="second", tag="bank0")
+        for g in range(G):
+            multiply(second[:], g, last_tile, EDGES[4], M, g == 0, g == G - 1)
+        finish(second[:], last_tile, EDGES[4], M)

from contextlib import ExitStack

import concourse.mybir as mybir
from concourse.masks import make_identity

G, K, M, T, S = 5, 512, 1024, 4096, 512
FLOPS = 2 * G * K * M * S

F32 = mybir.dt.float32
BF16 = mybir.dt.bfloat16
I32 = mybir.dt.int32
U32 = mybir.dt.uint32
U16 = mybir.dt.uint16
U8 = mybir.dt.uint8
FP8X4 = mybir.dt.float8_e4m3fn_x4
SILU = mybir.ActivationFunctionType.Silu
ADD = mybir.AluOpType.add

P = 128
PACK = 4
BANK = 512
TILES = S // P
GROUP = 16

EDGES = (0, 128, 256, 512, 768, 1024)
EARLY = G - 1


def tile_list_tabbag_tm_silu_kernel(tc, tab, w, b, offs, out):
    nc = tc.nc
    with ExitStack() as ctx:
        keep = ctx.enter_context(tc.tile_pool(name="keep", bufs=1))
        staged = ctx.enter_context(tc.tile_pool(name="staged", bufs=1))
        psum = ctx.enter_context(tc.psum_pool(name="psum", bufs=1))

        def sb(name, shape, dtype, at=None):
            if at is None:
                return keep.tile(shape, dtype, name=name, align_bytes=64)
            return staged.tile(shape, dtype, name=name, offset=at, align_bytes=64)

        def chunk_at(c):
            return 4 * PACK * EDGES[c]

        offsets = keep.tile([P, G * S // GROUP], U16, name="offsets")
        nc.sync.dma_start(offsets[:], offs)

        table_scales = sb("table_scales", [P, T], U8)
        nc.gpsimd.memset(table_scales[:, : T // 2].bitcast(I32), 0)
        nc.vector.memset(table_scales[:, T // 2 :].bitcast(I32), 0)
        ident = sb("ident", [P, P], F32)
        nc.vector.memset(ident[:], 0.0)
        make_identity(nc, ident[:], nomemset=True)

        b_run = M // P
        b_cols = sb("b_cols", [P, b_run], F32)
        nc.sync.dma_start(b_cols[:], b.rearrange("(p c) -> p c", c=b_run))

        w_rows = w.rearrange("(p i) n -> p i n", i=PACK)

        def load_w(c):
            raw = sb("w_raw%d" % c, [P, PACK, EDGES[c + 1] - EDGES[c]], F32, chunk_at(c))
            nc.sync.dma_start(raw[:], w_rows[:, :, EDGES[c] : EDGES[c + 1]])
            return raw

        scale_rows = tab[0, K * T :].rearrange("(q t) -> q t", t=T).bitcast(I32)
        for r in range(4):
            nc.sync.dma_start(table_scales[r:P:32, :].bitcast(I32), scale_rows[r:16:4, :])
        table_words = sb("table_words", [P, T], U32)
        nc.sync.dma_start(table_words[:].bitcast(I32), tab[0, : K * T].rearrange("(p c) -> p c", p=P).bitcast(I32))
        raws = [load_w(c) for c in range(len(EDGES) - 1)]

        w_words = sb("w_words", [P, M], U32)
        w_scales = sb("w_scales", [P, M], U8)

        def prepare_w(c):
            cols = slice(EDGES[c], EDGES[c + 1])
            rounded = sb("w_bf%d" % c, [P, (EDGES[c + 1] - EDGES[c]) * PACK], BF16)
            nc.scalar.copy(rounded[:].rearrange("p (n i) -> p n i", i=PACK), raws[c][:].rearrange("p i n -> p n i"))
            nc.vector.quantize_mx(out=w_words[:, cols].bitcast(FP8X4), scales=w_scales[:, cols], in_=rounded[:])

        def gather(name, window, dtype, m0, m1, at=None):
            picked = sb(name, [P, m1 - m0], dtype, at)
            nc.vector.tensor_copy(picked[:], window[:].indirect(offsets[:, m0 // GROUP : m1 // GROUP]))
            return picked

        picked_words = []

        def gather_words(g, at=None):
            picked_words.append(gather("words%d" % g, table_words, U32, g * S, (g + 1) * S, at))

        picked_scales = [gather("scales_early", table_scales, U8, 0, EARLY * S)]

        bias = sb("bias", [P, M], F32)
        per_bank = BANK // P
        for part in range(b_run // per_bank):
            spread = psum.tile([P, per_bank, P], F32, name="spread%d" % part, tag="bank%d" % (2 * TILES - 2 + part))
            for c in range(per_bank):
                col = per_bank * part + c
                nc.tensor.transpose(spread[:, c, :], b_cols[:, col : col + 1].to_broadcast([P, P]), ident[:])
            nc.scalar.copy(
                bias[:].rearrange("j (p c) -> j p c", c=b_run)[:, :, per_bank * part : per_bank * (part + 1)],
                spread[:].rearrange("j c p -> j p c"),
            )

        banks = [psum.tile([P, BANK], F32, name="acc%d" % i, tag="bank%d" % i) for i in range(2 * TILES)]

        def multiply(acc, g, t, n0, n1, opens, closes):
            m = (g % EARLY) * S + t * P
            nc.tensor.matmul_mx(
                out=acc,
                lhsT=picked_words[g][:, t * P : (t + 1) * P].bitcast(FP8X4),
                lhsT_scale=picked_scales[g // EARLY][:, m : m + P],
                rhs=w_words[:, n0:n1].bitcast(FP8X4),
                rhs_scale=w_scales[:, n0:n1],
                start=opens,
                stop=closes,
            )

        def into_bank(g, t, n0, n1, closes=False):
            half = n0 // BANK
            acc = banks[TILES * half + t][:, n0 - half * BANK : n1 - half * BANK]
            multiply(acc, g, t, n0, n1, g == 0 and n0 % BANK == 0, closes)

        def sweep(lookups, n0, n1, tiles=range(TILES)):
            for g in lookups:
                for t in tiles:
                    into_bank(g, t, n0, n1)

        def finish(acc, t, n0, n1):
            pre = sb("pre%d_%d" % (t, n0), [P, n1 - n0], F32)
            nc.vector.tensor_tensor(pre[:], acc, bias[:, n0:n1], ADD)
            res = sb("res%d_%d" % (t, n0), [P, n1 - n0], F32)
            nc.scalar.activation(res[:], pre[:], SILU)
            nc.sync.dma_start(out[t * P : (t + 1) * P, n0:n1], res[:])

        last_tile = TILES - 1
        gather_words(0)
        prepare_w(0)
        sweep([0], EDGES[0], EDGES[1])
        gather_words(1, chunk_at(0))
        sweep([1], EDGES[0], EDGES[1])
        prepare_w(1)
        sweep([0, 1], EDGES[1], EDGES[2])
        gather_words(2, chunk_at(1))
        sweep([2], EDGES[0], EDGES[2])
        prepare_w(2)
        sweep([0, 1, 2], EDGES[2], EDGES[3])
        gather_words(3, chunk_at(2))
        sweep([3], 0, BANK)
        prepare_w(3)
        sweep(range(G - 1), EDGES[3], EDGES[4], range(last_tile))
        picked_scales.append(gather("scales_late", table_scales, U8, EARLY * S, G * S, chunk_at(3)))
        prepare_w(4)
        gather_words(4, chunk_at(4))

        def close(i):
            half, t = divmod(i, TILES)
            into_bank(G - 1, t, half * BANK, (half + 1) * BANK, True)
            finish(banks[i][:], t, half * BANK, (half + 1) * BANK)

        for t in range(last_tile):
            close(2 * t)
            close(2 * t + 1)
            sweep(range(G - 1), EDGES[4], M, [t])
        close(2 * last_tile)

        for g in range(G):
            into_bank(g, last_tile, BANK, EDGES[4], g == G - 1)
        finish(banks[-1][:, : EDGES[4] - BANK], last_tile, BANK, EDGES[4])
        second = psum.tile([P, M - EDGES[4]], F32, name="second", tag="bank0")
        for g in range(G):
            multiply(second[:], g, last_tile, EDGES[4], M, g == 0, g == G - 1)
        finish(second[:], last_tile, EDGES[4], M)
